import numpy as np
import ml_dtypes


def mxq(x, axis, fmt="e4m3"):
    dtype, down = {"e4m3": (ml_dtypes.float8_e4m3fn, 7), "e5m2": (ml_dtypes.float8_e5m2, 14)}[fmt]
    v = np.moveaxis(np.asarray(x, np.float32).astype(ml_dtypes.bfloat16).astype(np.float64), axis, -1)
    blocks = v.reshape(v.shape[:-1] + (-1, 32))
    amax = np.abs(blocks).max(-1, keepdims=True)
    byte = np.maximum(np.where(amax > 0, np.frexp(amax)[1] - 1 + 127, 0) - down, 1)
    scale = np.exp2(byte - 127.0)
    codes = (blocks / scale).astype(np.float32).astype(dtype).astype(np.float64)
    return np.moveaxis((codes * scale).reshape(v.shape), -1, axis)


WIDE = False


def mx_kscale(k):
    if not WIDE:
        return np.ones(k)
    levels = np.array([10, -10, 5, -5, 0])
    if k % 512:
        return np.exp2(np.random.permutation(np.resize(levels, k // 32))).repeat(32)
    a = np.empty((k // 512, 16))
    for p in range(k // 512):
        a[p, :8] = np.random.permutation(np.resize(levels, 8))
        for g in range(8):
            far = levels[np.abs(levels - a[p, g]) >= 10]
            a[p, g + 8] = far[np.random.randint(len(far))]
    return np.exp2(a.ravel()).repeat(32)


def f64(x):
    return np.asarray(x).astype(np.float64)


def striped(idx):
    return np.tile(idx.reshape(-1, 16).T, (8, 1)).astype(np.uint16)


def unstriped(offs):
    return offs[:16].T.reshape(-1).astype(np.int64)


def striped8(idx):
    return np.concatenate([x.reshape(-1, 16).T for x in idx]).astype(np.uint16)


def runs(offs, k):
    lists = np.stack([offs[16 * r : 16 * r + 16].T.reshape(-1) for r in range(8)]).astype(np.int64)
    return lists[np.arange(k) % 512 // 64]


def pack_weight(w):
    k, n = w.shape
    w = f64(np.asarray(w, np.float32).astype(ml_dtypes.bfloat16)).reshape(k // 32, 32, n)
    amax = np.abs(w).max(1)
    byte = np.clip(np.where(amax > 0, np.frexp(amax)[1] - 1 + 127 - 7, 1), 1, 254)
    scaled = (w * np.exp2(127.0 - byte)[:, None, :]).reshape(k, n).astype(np.float32)
    words = np.ascontiguousarray(scaled.reshape(k // 512, 128, 4, n).transpose(0, 1, 3, 2)).astype(ml_dtypes.float8_e4m3fn).view(np.uint8)
    return words, np.ascontiguousarray(byte.astype(np.uint8).reshape(k // 512, 16, n))


def unpack_weight(words, scales):
    g, p, n, _ = words.shape
    vals = np.ascontiguousarray(words).view(ml_dtypes.float8_e4m3fn).astype(np.float64) * np.repeat(np.exp2(scales.astype(np.float64) - 127.0), 8, axis=1)[..., None]
    return vals.transpose(0, 1, 3, 2).reshape(g * 512, n)


K, T, S, N, G, H, J = 512, 2048, 512, 512, 2048, 512, 512


def setup_inputs():
    n = np.random.standard_normal
    s = mx_kscale(K)[:, None]
    u = mx_kscale(S)
    packed_xT = pack_weight(n((K, T)) * s)
    packed_dT = pack_weight(n((K, G)) / s)
    return {
        "x_words": packed_xT[0],
        "x_scales": packed_xT[1],
        "d_words": packed_dT[0],
        "d_scales": packed_dT[1],
        "tab": np.random.uniform(0.4, 1.4, (H, J)).astype(np.float32),
        "gn": (np.random.uniform(0.5, 1.5, (H, 1)) * u[:, None]).astype(np.float32),
        "w1": (n((H, N)) / np.sqrt(H) / u[:, None]).astype(np.float32),
        "offs": striped8(np.random.randint(0, T, (8, S))),
        "k1": striped8(np.random.randint(0, G, (8, H))),
        "n1": striped8(np.random.randint(0, J, (8, S))),
        "n2": striped8(np.stack([np.random.permutation(S) for _ in range(8)])),
        "n3": striped(np.random.randint(0, S, G)),
    }


def reference(x_words, x_scales, d_words, d_scales, tab, gn, w1, offs, k1, n1, n2, n3):
    d_k1 = unpack_weight(d_words, d_scales)[np.arange(K)[:, None], runs(k1, K)]
    xq = unpack_weight(x_words, x_scales)[np.arange(K)[:, None], runs(offs, K)]
    h = 0.0625 * (d_k1.T @ xq)
    z = f64(gn) * (h * (f64(tab)[np.arange(H)[:, None], runs(n1, H)]) - (0.5 * (h[np.arange(H)[:, None], runs(n2, H)])))
    h2 = mxq(f64(w1), 0, "e4m3").T @ mxq(z, 0, "e4m3")
    mb = h2[:, unstriped(n3)]
    mx = mb.reshape(N, S, 4).max(axis=2)
    mn = mb.reshape(N, S, 4).min(axis=2)
    return mx * np.tanh(h2 - mn)

@@ -1,0 +1,224 @@
+from contextlib import ExitStack
+
+import concourse.mybir as mybir
+
+K, T, S, N, G, H, J = 512, 2048, 512, 512, 2048, 512, 512
+FLOPS = 2 * K * H * S + 2 * H * N * S
+
+F32 = mybir.dt.float32
+BF16 = mybir.dt.bfloat16
+I32 = mybir.dt.int32
+U32 = mybir.dt.uint32
+U16 = mybir.dt.uint16
+U8 = mybir.dt.uint8
+FP8X4 = mybir.dt.float8_e4m3fn_x4
+ALU = mybir.AluOpType
+ACT = mybir.ActivationFunctionType
+
+P = 128
+PACK = 4
+HALF = 256
+MEMBERS = 4
+SPARE = 528
+
+
+def tile_picked_hpqkindggtan_none_p_kernel(
+    tc, x_words, x_scales, d_words, d_scales, tab, gn, w1, offs, k1, n1, n2, n3, out
+):
+    nc = tc.nc
+    with ExitStack() as ctx:
+        lists = ctx.enter_context(tc.tile_pool(name="lists", bufs=1))
+        keep = ctx.enter_context(tc.tile_pool(name="keep", bufs=1))
+        ring = ctx.enter_context(tc.tile_pool(name="ring", bufs=2))
+        psum = ctx.enter_context(tc.psum_pool(name="psum", bufs=8))
+
+        def load_list(src, name):
+            t = lists.tile(list(src.shape), U16, name=name)
+            nc.sync.dma_start(t[:], src)
+            return t
+
+        def load_scales(src, name, tag, eng):
+            t = keep.tile([P, T], U8, name=name, tag=tag, align_bytes=64)
+            eng.memset(t[:].bitcast(I32), 0)
+            nc.sync.dma_start(t[0:P:8, :].bitcast(I32), src[0].bitcast(I32))
+            return t
+
+        def load_words(src, name, tag):
+            t = keep.tile([P, T], U32, name=name, tag=tag, align_bytes=64)
+            nc.sync.dma_start(t[:].bitcast(I32), src[0].rearrange("p n r -> p (n r)").bitcast(I32))
+            return t
+
+        d_bytes = load_scales(d_scales, "d_bytes", "slot_a", nc.vector)
+        x_bytes = load_scales(x_scales, "x_bytes", "slot_b", nc.gpsimd)
+        k1_t = load_list(k1, "k1_t")
+        offs_t = load_list(offs, "offs_t")
+        n1_t = load_list(n1, "n1_t")
+        n2_t = load_list(n2, "n2_t")
+        n3_t = load_list(n3, "n3_t")
+        d_table = load_words(d_words, "d_table", "slot_c")
+        x_table = load_words(x_words, "x_table", "slot_d")
+
+        planes = keep.tile([P, H + S], U8, name="planes", align_bytes=64)
+        nc.gpsimd.memset(planes[:].bitcast(I32), 0)
+        gain = keep.tile([P, PACK], F32, name="gain")
+        nc.gpsimd.dma_start(gain[:], gn.rearrange("(p t) o -> p (t o)", t=PACK))
+        gain16 = keep.tile([P, PACK], F32, name="gain16")
+        nc.gpsimd.tensor_scalar(gain16[:], gain[:], 0.0625, 0.0, ALU.mult, ALU.add)
+
+        h2_rows = [keep.tile([P, S + SPARE], F32, name="h2_rows%d" % m) for m in range(N // P)]
+        for m in range(N // P):
+            nc.gpsimd.memset(h2_rows[m][:, S:], 0.0)
+
+        picked_bytes = keep.tile([P, H + S], U8, name="picked_bytes", tag="slot_e", align_bytes=64)
+        nc.vector.tensor_copy(picked_bytes[:, :H], d_bytes[:].indirect(k1_t[:]))
+        nc.vector.tensor_copy(picked_bytes[:, H:], x_bytes[:].indirect(offs_t[:]))
+        for q in range(4):
+            nc.scalar.dma_start(
+                planes[32 * q : 32 * q + 4, :].bitcast(I32), picked_bytes[32 * q : 32 * q + 32 : 8, :].bitcast(I32)
+            )
+
+        tab_rows = tab.rearrange("(p t) n -> p t n", t=PACK)
+
+        def load_tab(t, tag):
+            tile = keep.tile([P, J], F32, name="tab%d" % t, tag=tag, align_bytes=64)
+            nc.sync.dma_start(tile[:], tab_rows[:, t, :])
+            return tile
+
+        tab_t = [load_tab(0, "slot_a")]
+
+        d_picked = keep.tile([P, H], U32, name="d_picked", tag="slot_b", align_bytes=64)
+        nc.vector.tensor_copy(d_picked[:], d_table[:].indirect(k1_t[:]))
+        tab_t.append(load_tab(1, "slot_c"))
+        d_dealt = keep.tile([P, H], U32, name="d_dealt", align_bytes=64)
+        nc.vector.tensor_copy(
+            d_dealt[:].bitcast(I32).rearrange("p (t c i) -> p c t i", t=PACK, i=4),
+            d_picked[:].bitcast(I32).rearrange("p (c i t) -> p c t i", t=PACK, i=4),
+        )
+        w_raw = keep.tile([P, PACK, N], F32, name="w_raw", tag="slot_b", align_bytes=64)
+        nc.sync.dma_start(w_raw[:], w1.rearrange("(p t) n -> p t n", t=PACK))
+        x_picked = keep.tile([P, S], U32, name="x_picked", align_bytes=64)
+        nc.vector.tensor_copy(x_picked[:], x_table[:].indirect(offs_t[:]))
+        d_plane = keep.tile([P, H], U8, name="d_plane", tag="slot_d", align_bytes=64)
+        nc.vector.tensor_copy(
+            d_plane[:].rearrange("p (t c i) -> p c t i", t=PACK, i=16),
+            planes[:, :H].rearrange("p (c i t) -> p c t i", t=PACK, i=16),
+        )
+        tab_t.append(load_tab(2, "slot_e"))
+
+        h_banks = []
+        for t in range(PACK):
+            bank = psum.tile([P, S], F32, name="bank", tag="bank")
+            cols = slice(t * P, (t + 1) * P)
+            nc.tensor.matmul_mx(
+                out=bank[:], lhsT=d_dealt[:, cols].bitcast(FP8X4), lhsT_scale=d_plane[:, cols],
+                rhs=x_picked[:].bitcast(FP8X4), rhs_scale=planes[:, H:], start=True, stop=True,
+            )
+            h_banks.append(bank)
+
+        halves = S // HALF
+        lcols = HALF // 16
+        EARLY = 2
+        tab_picked = [keep.tile([P, S], F32, name="tab_picked%d" % t) for t in range(EARLY)]
+        u_rows = [keep.tile([P, S], F32, name="u_rows%d" % t) for t in range(PACK)]
+        gated = keep.tile([P, PACK, S], F32, name="gated")
+        u_picked = [keep.tile([P, PACK, HALF], F32, name="u_picked%d" % c) for c in range(halves)]
+
+        for t in range(EARLY):
+            for c in range(halves):
+                nc.scalar.activation(
+                    tab_picked[t][:, c * HALF : (c + 1) * HALF],
+                    tab_t[t][:].indirect(n1_t[:, c * lcols : (c + 1) * lcols]), ACT.Copy,
+                )
+            if t == 0:
+                tab_t.append(load_tab(3, "slot_a"))
+            nc.vector.scalar_tensor_tensor(
+                gated[:, t, :], h_banks[t][:], gain16[:, t : t + 1], tab_picked[t][:], ALU.mult, ALU.mult
+            )
+        for t in [2, 3, 0, 1]:
+            nc.scalar.activation(u_rows[t][:], h_banks[t][:], ACT.Copy, scale=gain16[:, t : t + 1])
+        for c in range(halves):
+            for t in range(PACK):
+                nc.scalar.activation(
+                    u_picked[c][:, t, :], u_rows[t][:].indirect(n2_t[:, c * lcols : (c + 1) * lcols]),
+                    ACT.Copy, scale=-0.5,
+                )
+        for c in range(halves):
+            for t in range(EARLY, PACK):
+                cols = slice(c * HALF, (c + 1) * HALF)
+                nc.vector.tensor_tensor(
+                    gated[:, t, cols], tab_t[t][:].indirect(n1_t[:, c * lcols : (c + 1) * lcols]),
+                    u_rows[t][:, cols], ALU.mult,
+                )
+
+        w_grouped = keep.tile([P, N * PACK], BF16, name="w_grouped", align_bytes=64)
+        nc.vector.tensor_copy(
+            w_grouped[:].rearrange("p (c i t) -> p c t i", t=PACK, i=4),
+            w_raw[:].rearrange("p t (c i) -> p c t i", i=4),
+        )
+        w_codes = keep.tile([P, N], U32, name="w_codes", align_bytes=64)
+        w_plane = keep.tile([P, N], U8, name="w_plane", align_bytes=64)
+        nc.vector.quantize_mx(out=w_codes[:].bitcast(FP8X4), scales=w_plane[:], in_=w_grouped[:])
+
+        for c in range(halves):
+            cols = slice(c * HALF, (c + 1) * HALF)
+            z_grouped = ring.tile([P, HALF * PACK], BF16, name="z_grouped", align_bytes=64)
+            nc.vector.tensor_tensor(
+                z_grouped[:].rearrange("p (c i t) -> p c t i", t=PACK, i=2),
+                u_picked[c][:].rearrange("p t (c i) -> p c t i", i=2),
+                gated[:, :, cols].rearrange("p t (c i) -> p c t i", i=2),
+                ALU.add,
+            )
+            z_codes = ring.tile([P, HALF], U32, name="z_codes", align_bytes=64)
+            z_plane = ring.tile([P, HALF], U8, name="z_plane", align_bytes=64)
+            nc.vector.quantize_mx(out=z_codes[:].bitcast(FP8X4), scales=z_plane[:], in_=z_grouped[:])
+            for m in range(N // P):
+                bank = psum.tile([P, HALF], F32, name="bank", tag="bank")
+                rows = slice(m * P, (m + 1) * P)
+                nc.tensor.matmul_mx(
+                    out=bank[:], lhsT=w_codes[:, rows].bitcast(FP8X4), lhsT_scale=w_plane[:, rows],
+                    rhs=z_codes[:].bitcast(FP8X4), rhs_scale=z_plane[:], start=True, stop=True,
+                )
+                nc.scalar.activation(h2_rows[m][:, cols], bank[:], ACT.Copy)
+
+        QUART = 128
+        chunks = []
+        for m in range(N // P):
+            if m < N // P - 1:
+                chunks.extend([(m, 0, HALF), (m, HALF, HALF)])
+            else:
+                chunks.extend([(m, 0, HALF), (m, HALF, QUART), (m, HALF + QUART, QUART)])
+        shared = [(0, 0), (1, 0)]
+
+        def finish(state):
+            m, j0, w, mx, th = state
+            res = ring.tile([P, w], F32, name="res", tag="res", bufs=3)
+            nc.vector.tensor_tensor(res[:], mx[:], th[:], ALU.mult)
+            nc.sync.dma_start(out[m * P : (m + 1) * P, j0 : j0 + w], res[:])
+
+        pending = None
+        for m, j0, w in chunks:
+            mb = ring.tile([P, w * MEMBERS], F32, name="mb", tag="mb")
+            c0, c1 = j0 * MEMBERS // 16, (j0 + w) * MEMBERS // 16
+            if (m, j0) in shared:
+                mid = (c0 + c1) // 2
+                nc.scalar.activation(mb[:, : w * 2], h2_rows[m][:].indirect(n3_t[:, c0:mid]), ACT.Copy)
+                nc.vector.tensor_copy(mb[:, w * 2 :], h2_rows[m][:].indirect(n3_t[:, mid:c1]))
+            else:
+                nc.scalar.activation(mb[:], h2_rows[m][:].indirect(n3_t[:, c0:c1]), ACT.Copy)
+            quads = mb[:].rearrange("p (j a b) -> p j a b", a=2, b=2)
+            hi = ring.tile([P, w, 2], F32, name="hi", tag="hi")
+            lo = ring.tile([P, w, 2], F32, name="lo", tag="lo")
+            nc.vector.tensor_tensor(hi[:], quads[:, :, 0, :], quads[:, :, 1, :], ALU.max)
+            nc.vector.tensor_tensor(lo[:], quads[:, :, 0, :], quads[:, :, 1, :], ALU.min)
+            mx = ring.tile([P, w], F32, name="mx", tag="mx", bufs=3)
+            mn = ring.tile([P, w], F32, name="mn", tag="mn")
+            nc.vector.tensor_tensor(mn[:], lo[:, :, 0], lo[:, :, 1], ALU.min)
+            nc.vector.tensor_tensor(mx[:], hi[:, :, 0], hi[:, :, 1], ALU.max)
+            gap = ring.tile([P, w], F32, name="gap", tag="gap")
+            nc.vector.tensor_tensor(gap[:], h2_rows[m][:, j0 : j0 + w], mn[:], ALU.subtract)
+            if pending is not None:
+                finish(pending)
+            th = ring.tile([P, w], F32, name="th", tag="th")
+            nc.scalar.activation(th[:], gap[:], ACT.Tanh)
+            pending = (m, j0, w, mx, th)
+        finish(pending)

@@ -18,8 +18,11 @@ ACT = mybir.ActivationFunctionType
 P = 128
 PACK = 4
 HALF = 256
+QUARTER = 128
 MEMBERS = 4
-SPARE = 528
+PER_COLUMN = 16
+WINDOW = HALF * MEMBERS + PER_COLUMN
+TILES = N // P
 
 
 def tile_picked_hpqkindggtan_none_p_kernel(
@@ -32,193 +35,195 @@ def tile_picked_hpqkindggtan_none_p_kernel(
         ring = ctx.enter_context(tc.tile_pool(name="ring", bufs=2))
         psum = ctx.enter_context(tc.psum_pool(name="psum", bufs=8))
 
+        def held(shape, dtype, name, tag):
+            return keep.tile(shape, dtype, name=name, tag=tag, align_bytes=64)
+
+        def entries(list_tile, first, count):
+            return list_tile[:, first // PER_COLUMN : (first + count) // PER_COLUMN]
+
         def load_list(src, name):
-            t = lists.tile(list(src.shape), U16, name=name)
-            nc.sync.dma_start(t[:], src)
-            return t
-
-        def load_scales(src, name, tag, eng):
-            t = keep.tile([P, T], U8, name=name, tag=tag, align_bytes=64)
-            eng.memset(t[:].bitcast(I32), 0)
-            nc.sync.dma_start(t[0:P:8, :].bitcast(I32), src[0].bitcast(I32))
-            return t
-
-        def load_words(src, name, tag):
-            t = keep.tile([P, T], U32, name=name, tag=tag, align_bytes=64)
-            nc.sync.dma_start(t[:].bitcast(I32), src[0].rearrange("p n r -> p (n r)").bitcast(I32))
-            return t
-
-        d_bytes = load_scales(d_scales, "d_bytes", "slot_a", nc.vector)
-        x_bytes = load_scales(x_scales, "x_bytes", "slot_b", nc.gpsimd)
-        k1_t = load_list(k1, "k1_t")
-        offs_t = load_list(offs, "offs_t")
-        n1_t = load_list(n1, "n1_t")
-        n2_t = load_list(n2, "n2_t")
-        n3_t = load_list(n3, "n3_t")
-        d_table = load_words(d_words, "d_table", "slot_c")
-        x_table = load_words(x_words, "x_table", "slot_d")
-
-        planes = keep.tile([P, H + S], U8, name="planes", align_bytes=64)
-        nc.gpsimd.memset(planes[:].bitcast(I32), 0)
-        gain = keep.tile([P, PACK], F32, name="gain")
-        nc.gpsimd.dma_start(gain[:], gn.rearrange("(p t) o -> p (t o)", t=PACK))
-        gain16 = keep.tile([P, PACK], F32, name="gain16")
-        nc.gpsimd.tensor_scalar(gain16[:], gain[:], 0.0625, 0.0, ALU.mult, ALU.add)
-
-        h2_rows = [keep.tile([P, S + SPARE], F32, name="h2_rows%d" % m) for m in range(N // P)]
-        for m in range(N // P):
-            nc.gpsimd.memset(h2_rows[m][:, S:], 0.0)
-
-        picked_bytes = keep.tile([P, H + S], U8, name="picked_bytes", tag="slot_e", align_bytes=64)
-        nc.vector.tensor_copy(picked_bytes[:, :H], d_bytes[:].indirect(k1_t[:]))
-        nc.vector.tensor_copy(picked_bytes[:, H:], x_bytes[:].indirect(offs_t[:]))
-        for q in range(4):
-            nc.scalar.dma_start(
-                planes[32 * q : 32 * q + 4, :].bitcast(I32), picked_bytes[32 * q : 32 * q + 32 : 8, :].bitcast(I32)
-            )
-
-        tab_rows = tab.rearrange("(p t) n -> p t n", t=PACK)
-
-        def load_tab(t, tag):
-            tile = keep.tile([P, J], F32, name="tab%d" % t, tag=tag, align_bytes=64)
-            nc.sync.dma_start(tile[:], tab_rows[:, t, :])
+            tile = lists.tile(list(src.shape), U16, name=name)
+            nc.sync.dma_start(tile[:], src)
             return tile
 
-        tab_t = [load_tab(0, "slot_a")]
+        def load_scales(src, name, engine, queue):
+            tile = held([P, T], U8, name, name)
+            engine.memset(tile[:].bitcast(I32), 0)
+            queue.dma_start(tile[0:P:8, :].bitcast(I32), src[0].bitcast(I32))
+            return tile
 
-        d_picked = keep.tile([P, H], U32, name="d_picked", tag="slot_b", align_bytes=64)
-        nc.vector.tensor_copy(d_picked[:], d_table[:].indirect(k1_t[:]))
-        tab_t.append(load_tab(1, "slot_c"))
-        d_dealt = keep.tile([P, H], U32, name="d_dealt", align_bytes=64)
+        def load_words(src, name):
+            tile = held([P, T], U32, name, name)
+            nc.sync.dma_start(tile[:].bitcast(I32), src[0].rearrange("p n r -> p (n r)").bitcast(I32))
+            return tile
+
+        def load_tab(t, tag):
+            tile = held([P, J], F32, "tab%d" % t, tag)
+            nc.sync.dma_start(tile[:], tab.rearrange("(p t) n -> p t n", t=PACK)[:, t, :])
+            return tile
+
+        d_bytes = load_scales(d_scales, "d_bytes", nc.vector, nc.sync)
+        x_bytes = load_scales(x_scales, "x_bytes", nc.gpsimd, nc.scalar)
+        k1_list = load_list(k1, "k1_list")
+        offs_list = load_list(offs, "offs_list")
+        n1_list = load_list(n1, "n1_list")
+        n2_list = load_list(n2, "n2_list")
+        n3_list = load_list(n3, "n3_list")
+        d_table = load_words(d_words, "d_table")
+        tab_rows = [load_tab(0, "tab0"), load_tab(1, "tab1")]
+        x_table = load_words(x_words, "x_table")
+
+        planes = held([P, H + S], U8, "planes", "planes")
+        nc.gpsimd.memset(planes[:].bitcast(I32), 0)
+        gain = held([P, PACK], F32, "gain", "gain")
+        nc.gpsimd.dma_start(gain[:], gn.rearrange("(p t) o -> p (t o)", t=PACK))
+        gain16 = held([P, PACK], F32, "gain16", "gain16")
+        nc.gpsimd.tensor_scalar(gain16[:], gain[:], 0.0625, 0.0, ALU.mult, ALU.add)
+        h2_rows = [held([P, WINDOW], F32, "h2_rows%d" % m, "h2_rows%d" % m) for m in range(TILES)]
+        for m in range(TILES):
+            nc.gpsimd.memset(h2_rows[m][:, S:], 0.0)
+
+        picked_bytes = held([P, H + S], U8, "picked_bytes", "picked_bytes")
+        nc.vector.tensor_copy(picked_bytes[:, :H], d_bytes[:].indirect(k1_list[:]))
+        nc.vector.tensor_copy(picked_bytes[:, H:], x_bytes[:].indirect(offs_list[:]))
+        dealt_bytes = held([P, H + S], U8, "dealt_bytes", "dealt_bytes")
+        nc.vector.tensor_copy(
+            dealt_bytes[:, :H].rearrange("p (t c i) -> p c t i", t=PACK, i=16),
+            picked_bytes[:, :H].rearrange("p (c i t) -> p c t i", t=PACK, i=16),
+        )
+        nc.vector.tensor_copy(dealt_bytes[:, H:].bitcast(I32), picked_bytes[:, H:].bitcast(I32))
+        for q in range(4):
+            nc.sync.dma_start(
+                planes[32 * q : 32 * q + 4, :].bitcast(I32), dealt_bytes[32 * q : 32 * q + 32 : 8, :].bitcast(I32)
+            )
+
+        d_picked = held([P, H], U32, "d_picked", "picked_bytes")
+        nc.vector.tensor_copy(d_picked[:], d_table[:].indirect(k1_list[:]))
+        tab_rows.append(load_tab(2, "d_table"))
+        d_dealt = held([P, H], U32, "d_dealt", "d_dealt")
         nc.vector.tensor_copy(
             d_dealt[:].bitcast(I32).rearrange("p (t c i) -> p c t i", t=PACK, i=4),
             d_picked[:].bitcast(I32).rearrange("p (c i t) -> p c t i", t=PACK, i=4),
         )
-        w_raw = keep.tile([P, PACK, N], F32, name="w_raw", tag="slot_b", align_bytes=64)
+        tab_rows.append(load_tab(3, "picked_bytes"))
+        w_raw = held([P, PACK, N], F32, "w_raw", "dealt_bytes")
         nc.sync.dma_start(w_raw[:], w1.rearrange("(p t) n -> p t n", t=PACK))
-        x_picked = keep.tile([P, S], U32, name="x_picked", align_bytes=64)
-        nc.vector.tensor_copy(x_picked[:], x_table[:].indirect(offs_t[:]))
-        d_plane = keep.tile([P, H], U8, name="d_plane", tag="slot_d", align_bytes=64)
-        nc.vector.tensor_copy(
-            d_plane[:].rearrange("p (t c i) -> p c t i", t=PACK, i=16),
-            planes[:, :H].rearrange("p (c i t) -> p c t i", t=PACK, i=16),
-        )
-        tab_t.append(load_tab(2, "slot_e"))
+        x_picked = held([P, S], U32, "x_picked", "x_picked")
+        nc.vector.tensor_copy(x_picked[:], x_table[:].indirect(offs_list[:]))
 
         h_banks = []
         for t in range(PACK):
             bank = psum.tile([P, S], F32, name="bank", tag="bank")
             cols = slice(t * P, (t + 1) * P)
             nc.tensor.matmul_mx(
-                out=bank[:], lhsT=d_dealt[:, cols].bitcast(FP8X4), lhsT_scale=d_plane[:, cols],
+                out=bank[:], lhsT=d_dealt[:, cols].bitcast(FP8X4), lhsT_scale=planes[:, cols],
                 rhs=x_picked[:].bitcast(FP8X4), rhs_scale=planes[:, H:], start=True, stop=True,
             )
             h_banks.append(bank)
 
-        halves = S // HALF
-        lcols = HALF // 16
-        EARLY = 2
-        tab_picked = [keep.tile([P, S], F32, name="tab_picked%d" % t) for t in range(EARLY)]
-        u_rows = [keep.tile([P, S], F32, name="u_rows%d" % t) for t in range(PACK)]
-        gated = keep.tile([P, PACK, S], F32, name="gated")
-        u_picked = [keep.tile([P, PACK, HALF], F32, name="u_picked%d" % c) for c in range(halves)]
-
-        for t in range(EARLY):
-            for c in range(halves):
+        tab_picked = [held([P, S], F32, "tab_picked%d" % t, "tab_picked%d" % t) for t in range(PACK)]
+        for t in range(PACK):
+            for j0 in range(0, S, HALF):
                 nc.scalar.activation(
-                    tab_picked[t][:, c * HALF : (c + 1) * HALF],
-                    tab_t[t][:].indirect(n1_t[:, c * lcols : (c + 1) * lcols]), ACT.Copy,
+                    tab_picked[t][:, j0 : j0 + HALF], tab_rows[t][:].indirect(entries(n1_list, j0, HALF)), ACT.Copy
                 )
-            if t == 0:
-                tab_t.append(load_tab(3, "slot_a"))
+
+        g_tags = ["tab0", "tab1", "d_table", "d_bytes"]
+        g_rows = [held([P, S], F32, "g_rows%d" % t, g_tags[t]) for t in range(PACK)]
+        gated = held([P, PACK, S], F32, "gated", "gated")
+        for t in range(PACK):
+            if t < 4:
+                nc.vector.tensor_scalar(g_rows[t][:], h_banks[t][:], gain16[:, t : t + 1], None, ALU.mult)
+            else:
+                nc.scalar.activation(g_rows[t][:], h_banks[t][:], ACT.Copy, scale=gain16[:, t : t + 1])
+        for t in range(PACK):
             nc.vector.scalar_tensor_tensor(
                 gated[:, t, :], h_banks[t][:], gain16[:, t : t + 1], tab_picked[t][:], ALU.mult, ALU.mult
             )
-        for t in [2, 3, 0, 1]:
-            nc.scalar.activation(u_rows[t][:], h_banks[t][:], ACT.Copy, scale=gain16[:, t : t + 1])
-        for c in range(halves):
+        g_picked = [held([P, PACK, HALF], F32, "g_picked%d" % c, ["picked_bytes", "x_picked"][c]) for c in range(2)]
+        for c in range(2):
             for t in range(PACK):
                 nc.scalar.activation(
-                    u_picked[c][:, t, :], u_rows[t][:].indirect(n2_t[:, c * lcols : (c + 1) * lcols]),
+                    g_picked[c][:, t, :], g_rows[t][:].indirect(entries(n2_list, c * HALF, HALF)),
                     ACT.Copy, scale=-0.5,
                 )
-        for c in range(halves):
-            for t in range(EARLY, PACK):
-                cols = slice(c * HALF, (c + 1) * HALF)
-                nc.vector.tensor_tensor(
-                    gated[:, t, cols], tab_t[t][:].indirect(n1_t[:, c * lcols : (c + 1) * lcols]),
-                    u_rows[t][:, cols], ALU.mult,
-                )
 
-        w_grouped = keep.tile([P, N * PACK], BF16, name="w_grouped", align_bytes=64)
-        nc.vector.tensor_copy(
-            w_grouped[:].rearrange("p (c i t) -> p c t i", t=PACK, i=4),
-            w_raw[:].rearrange("p t (c i) -> p c t i", i=4),
+        w_grouped = held([P, N * PACK], BF16, "w_grouped", "grouped")
+        nc.gpsimd.tensor_scalar(
+            w_grouped[:].rearrange("p (n t) -> p n t", t=PACK), w_raw[:].rearrange("p t n -> p n t"),
+            1.0, 0.0, ALU.mult, ALU.add,
         )
-        w_codes = keep.tile([P, N], U32, name="w_codes", align_bytes=64)
-        w_plane = keep.tile([P, N], U8, name="w_plane", align_bytes=64)
+        w_codes = held([P, N], U32, "w_codes", "w_codes")
+        w_plane = held([P, N], U8, "w_plane", "w_plane")
         nc.vector.quantize_mx(out=w_codes[:].bitcast(FP8X4), scales=w_plane[:], in_=w_grouped[:])
 
-        for c in range(halves):
+        h2_banks = {}
+        for c in range(2):
             cols = slice(c * HALF, (c + 1) * HALF)
-            z_grouped = ring.tile([P, HALF * PACK], BF16, name="z_grouped", align_bytes=64)
+            z_grouped = held([P, HALF * PACK], BF16, "z_grouped", "grouped")
             nc.vector.tensor_tensor(
                 z_grouped[:].rearrange("p (c i t) -> p c t i", t=PACK, i=2),
-                u_picked[c][:].rearrange("p t (c i) -> p c t i", i=2),
+                g_picked[c][:].rearrange("p t (c i) -> p c t i", i=2),
                 gated[:, :, cols].rearrange("p t (c i) -> p c t i", i=2),
                 ALU.add,
             )
             z_codes = ring.tile([P, HALF], U32, name="z_codes", align_bytes=64)
             z_plane = ring.tile([P, HALF], U8, name="z_plane", align_bytes=64)
             nc.vector.quantize_mx(out=z_codes[:].bitcast(FP8X4), scales=z_plane[:], in_=z_grouped[:])
-            for m in range(N // P):
+            for m in range(TILES):
                 bank = psum.tile([P, HALF], F32, name="bank", tag="bank")
                 rows = slice(m * P, (m + 1) * P)
                 nc.tensor.matmul_mx(
                     out=bank[:], lhsT=w_codes[:, rows].bitcast(FP8X4), lhsT_scale=w_plane[:, rows],
                     rhs=z_codes[:].bitcast(FP8X4), rhs_scale=z_plane[:], start=True, stop=True,
                 )
-                nc.scalar.activation(h2_rows[m][:, cols], bank[:], ACT.Copy)
+                h2_banks[(m, c)] = bank
 
-        QUART = 128
-        chunks = []
-        for m in range(N // P):
-            if m < N // P - 1:
-                chunks.extend([(m, 0, HALF), (m, HALF, HALF)])
-            else:
-                chunks.extend([(m, 0, HALF), (m, HALF, QUART), (m, HALF + QUART, QUART)])
+        def evict(m, c):
+            nc.scalar.activation(h2_rows[m][:, c * HALF : (c + 1) * HALF], h2_banks[(m, c)][:], ACT.Copy)
+
+        for m in range(TILES):
+            evict(m, 0)
+        evict(0, 1)
+
+        steps = [(m, j0, HALF) for m in range(TILES) for j0 in (0, HALF)][:-1]
+        steps.extend([(TILES - 1, HALF, QUARTER), (TILES - 1, HALF + QUARTER, QUARTER)])
         shared = [(0, 0), (1, 0)]
 
-        def finish(state):
-            m, j0, w, mx, th = state
-            res = ring.tile([P, w], F32, name="res", tag="res", bufs=3)
-            nc.vector.tensor_tensor(res[:], mx[:], th[:], ALU.mult)
-            nc.sync.dma_start(out[m * P : (m + 1) * P, j0 : j0 + w], res[:])
+        def finish(m, j0, width, largest, squashed):
+            result = ring.tile([P, width], F32, name="result", tag="result", bufs=3)
+            nc.vector.tensor_tensor(result[:], largest[:], squashed[:], ALU.mult)
+            nc.sync.dma_start(out[m * P : (m + 1) * P, j0 : j0 + width], result[:])
 
         pending = None
-        for m, j0, w in chunks:
-            mb = ring.tile([P, w * MEMBERS], F32, name="mb", tag="mb")
-            c0, c1 = j0 * MEMBERS // 16, (j0 + w) * MEMBERS // 16
+        for m, j0, width in steps:
+            if j0 == 0 and m + 1 < TILES:
+                evict(m + 1, 1)
+            count = width * MEMBERS
+            first = j0 * MEMBERS
+            members = ring.tile([P, count], F32, name="members", tag="members")
             if (m, j0) in shared:
-                mid = (c0 + c1) // 2
-                nc.scalar.activation(mb[:, : w * 2], h2_rows[m][:].indirect(n3_t[:, c0:mid]), ACT.Copy)
-                nc.vector.tensor_copy(mb[:, w * 2 :], h2_rows[m][:].indirect(n3_t[:, mid:c1]))
+                part = count // 2
+                nc.scalar.activation(
+                    members[:, :part], h2_rows[m][:].indirect(entries(n3_list, first, part)), ACT.Copy
+                )
+                nc.vector.tensor_copy(members[:, part:], h2_rows[m][:].indirect(entries(n3_list, first + part, part)))
             else:
-                nc.scalar.activation(mb[:], h2_rows[m][:].indirect(n3_t[:, c0:c1]), ACT.Copy)
-            quads = mb[:].rearrange("p (j a b) -> p j a b", a=2, b=2)
-            hi = ring.tile([P, w, 2], F32, name="hi", tag="hi")
-            lo = ring.tile([P, w, 2], F32, name="lo", tag="lo")
-            nc.vector.tensor_tensor(hi[:], quads[:, :, 0, :], quads[:, :, 1, :], ALU.max)
-            nc.vector.tensor_tensor(lo[:], quads[:, :, 0, :], quads[:, :, 1, :], ALU.min)
-            mx = ring.tile([P, w], F32, name="mx", tag="mx", bufs=3)
-            mn = ring.tile([P, w], F32, name="mn", tag="mn")
-            nc.vector.tensor_tensor(mn[:], lo[:, :, 0], lo[:, :, 1], ALU.min)
-            nc.vector.tensor_tensor(mx[:], hi[:, :, 0], hi[:, :, 1], ALU.max)
-            gap = ring.tile([P, w], F32, name="gap", tag="gap")
-            nc.vector.tensor_tensor(gap[:], h2_rows[m][:, j0 : j0 + w], mn[:], ALU.subtract)
+                nc.scalar.activation(members[:], h2_rows[m][:].indirect(entries(n3_list, first, count)), ACT.Copy)
+            quads = members[:].rearrange("p (j a b) -> p j a b", a=2, b=2)
+            high = ring.tile([P, width, 2], F32, name="high", tag="high")
+            low = ring.tile([P, width, 2], F32, name="low", tag="low")
+            nc.vector.tensor_tensor(high[:], quads[:, :, 0, :], quads[:, :, 1, :], ALU.max)
+            nc.vector.tensor_tensor(low[:], quads[:, :, 0, :], quads[:, :, 1, :], ALU.min)
+            largest = ring.tile([P, width], F32, name="largest", tag="largest", bufs=3)
+            smallest = ring.tile([P, width], F32, name="smallest", tag="smallest")
+            nc.vector.tensor_tensor(largest[:], high[:, :, 0], high[:, :, 1], ALU.max)
+            nc.vector.tensor_tensor(smallest[:], low[:, :, 0], low[:, :, 1], ALU.min)
             if pending is not None:
-                finish(pending)
-            th = ring.tile([P, w], F32, name="th", tag="th")
-            nc.scalar.activation(th[:], gap[:], ACT.Tanh)
-            pending = (m, j0, w, mx, th)
-        finish(pending)
+                finish(*pending)
+            gap = ring.tile([P, width], F32, name="gap", tag="gap")
+            nc.vector.tensor_tensor(gap[:], h2_rows[m][:, j0 : j0 + width], smallest[:], ALU.subtract)
+            squashed = ring.tile([P, width], F32, name="squashed", tag="squashed")
+            nc.scalar.activation(squashed[:], gap[:], ACT.Tanh)
+            pending = (m, j0, width, largest, squashed)
+        finish(*pending)

@@ -21,7 +21,8 @@ HALF = 256
 QUARTER = 128
 MEMBERS = 4
 PER_COLUMN = 16
-WINDOW = HALF * MEMBERS + PER_COLUMN
+PICK = QUARTER * MEMBERS
+WINDOW = PICK + PER_COLUMN
 TILES = N // P
 
 
@@ -132,7 +133,7 @@ def tile_picked_hpqkindggtan_none_p_kernel(
         g_rows = [held([P, S], F32, "g_rows%d" % t, g_tags[t]) for t in range(PACK)]
         gated = held([P, PACK, S], F32, "gated", "gated")
         for t in range(PACK):
-            if t < 4:
+            if t < 3:
                 nc.vector.tensor_scalar(g_rows[t][:], h_banks[t][:], gain16[:, t : t + 1], None, ALU.mult)
             else:
                 nc.scalar.activation(g_rows[t][:], h_banks[t][:], ACT.Copy, scale=gain16[:, t : t + 1])
@@ -188,7 +189,7 @@ def tile_picked_hpqkindggtan_none_p_kernel(
 
         steps = [(m, j0, HALF) for m in range(TILES) for j0 in (0, HALF)][:-1]
         steps.extend([(TILES - 1, HALF, QUARTER), (TILES - 1, HALF + QUARTER, QUARTER)])
-        shared = [(0, 0), (1, 0)]
+        shared = [(0, 1), (1, 1)]
 
         def finish(m, j0, width, largest, squashed):
             result = ring.tile([P, width], F32, name="result", tag="result", bufs=3)
@@ -202,14 +203,12 @@ def tile_picked_hpqkindggtan_none_p_kernel(
             count = width * MEMBERS
             first = j0 * MEMBERS
             members = ring.tile([P, count], F32, name="members", tag="members")
-            if (m, j0) in shared:
-                part = count // 2
-                nc.scalar.activation(
-                    members[:, :part], h2_rows[m][:].indirect(entries(n3_list, first, part)), ACT.Copy
-                )
-                nc.vector.tensor_copy(members[:, part:], h2_rows[m][:].indirect(entries(n3_list, first + part, part)))
-            else:
-                nc.scalar.activation(members[:], h2_rows[m][:].indirect(entries(n3_list, first, count)), ACT.Copy)
+            for at in range(0, count, PICK):
+                picked = h2_rows[m][:].indirect(entries(n3_list, first + at, PICK))
+                if (m, (first + at) // PICK) in shared:
+                    nc.vector.tensor_copy(members[:, at : at + PICK], picked)
+                else:
+                    nc.scalar.activation(members[:, at : at + PICK], picked, ACT.Copy)
             quads = members[:].rearrange("p (j a b) -> p j a b", a=2, b=2)
             high = ring.tile([P, width, 2], F32, name="high", tag="high")
             low = ring.tile([P, width, 2], F32, name="low", tag="low")

@@ -73,6 +73,7 @@ def tile_picked_hpqkindggtan_none_p_kernel(
         d_table = load_words(d_words, "d_table")
         tab_rows = [load_tab(0, "tab0"), load_tab(1, "tab1")]
         x_table = load_words(x_words, "x_table")
+        tab_rows.append(load_tab(2, "tab2"))
 
         planes = held([P, H + S], U8, "planes", "planes")
         nc.gpsimd.memset(planes[:].bitcast(I32), 0)
@@ -98,29 +99,28 @@ def tile_picked_hpqkindggtan_none_p_kernel(
                 planes[32 * q : 32 * q + 4, :].bitcast(I32), dealt_bytes[32 * q : 32 * q + 32 : 8, :].bitcast(I32)
             )
 
+        tab_rows.append(load_tab(3, "x_bytes"))
         d_picked = held([P, H], U32, "d_picked", "picked_bytes")
         nc.vector.tensor_copy(d_picked[:], d_table[:].indirect(k1_list[:]))
-        tab_rows.append(load_tab(2, "d_table"))
+        w_raw = held([P, PACK, N], F32, "w_raw", "d_table")
+        nc.sync.dma_start(w_raw[:], w1.rearrange("(p t) n -> p t n", t=PACK))
         d_dealt = held([P, H], U32, "d_dealt", "d_dealt")
         nc.vector.tensor_copy(
             d_dealt[:].bitcast(I32).rearrange("p (t c i) -> p c t i", t=PACK, i=4),
             d_picked[:].bitcast(I32).rearrange("p (c i t) -> p c t i", t=PACK, i=4),
         )
-        tab_rows.append(load_tab(3, "picked_bytes"))
-        w_raw = held([P, PACK, N], F32, "w_raw", "dealt_bytes")
-        nc.sync.dma_start(w_raw[:], w1.rearrange("(p t) n -> p t n", t=PACK))
         x_picked = held([P, S], U32, "x_picked", "x_picked")
-        nc.vector.tensor_copy(x_picked[:], x_table[:].indirect(offs_list[:]))
+        for j0 in range(0, S, HALF):
+            nc.vector.tensor_copy(x_picked[:, j0 : j0 + HALF], x_table[:].indirect(entries(offs_list, j0, HALF)))
 
-        h_banks = []
-        for t in range(PACK):
-            bank = psum.tile([P, S], F32, name="bank", tag="bank")
+        h_banks = [psum.tile([P, S], F32, name="bank", tag="bank") for t in range(PACK)]
+        for t, j0 in [(0, 0), (1, 0), (0, HALF), (1, HALF), (2, 0), (2, HALF), (3, 0), (3, HALF)]:
             cols = slice(t * P, (t + 1) * P)
             nc.tensor.matmul_mx(
-                out=bank[:], lhsT=d_dealt[:, cols].bitcast(FP8X4), lhsT_scale=planes[:, cols],
-                rhs=x_picked[:].bitcast(FP8X4), rhs_scale=planes[:, H:], start=True, stop=True,
+                out=h_banks[t][:, j0 : j0 + HALF], lhsT=d_dealt[:, cols].bitcast(FP8X4), lhsT_scale=planes[:, cols],
+                rhs=x_picked[:, j0 : j0 + HALF].bitcast(FP8X4), rhs_scale=planes[:, H + j0 : H + j0 + HALF],
+                start=True, stop=True,
             )
-            h_banks.append(bank)
 
         tab_picked = [held([P, S], F32, "tab_picked%d" % t, "tab_picked%d" % t) for t in range(PACK)]
         for t in range(PACK):
@@ -129,19 +129,22 @@ def tile_picked_hpqkindggtan_none_p_kernel(
                     tab_picked[t][:, j0 : j0 + HALF], tab_rows[t][:].indirect(entries(n1_list, j0, HALF)), ACT.Copy
                 )
 
-        g_tags = ["tab0", "tab1", "d_table", "d_bytes"]
+        g_tags = ["x_bytes", "tab0", "tab1", "tab2"]
         g_rows = [held([P, S], F32, "g_rows%d" % t, g_tags[t]) for t in range(PACK)]
         gated = held([P, PACK, S], F32, "gated", "gated")
-        for t in range(PACK):
-            if t < 3:
-                nc.vector.tensor_scalar(g_rows[t][:], h_banks[t][:], gain16[:, t : t + 1], None, ALU.mult)
-            else:
-                nc.scalar.activation(g_rows[t][:], h_banks[t][:], ACT.Copy, scale=gain16[:, t : t + 1])
-        for t in range(PACK):
+
+        def gate(t):
             nc.vector.scalar_tensor_tensor(
                 gated[:, t, :], h_banks[t][:], gain16[:, t : t + 1], tab_picked[t][:], ALU.mult, ALU.mult
             )
-        g_picked = [held([P, PACK, HALF], F32, "g_picked%d" % c, ["picked_bytes", "x_picked"][c]) for c in range(2)]
+
+        gate(0)
+        nc.scalar.activation(g_rows[0][:], h_banks[0][:], ACT.Copy, scale=gain16[:, 0:1])
+        for t in range(1, PACK):
+            nc.vector.tensor_scalar(g_rows[t][:], h_banks[t][:], gain16[:, t : t + 1], None, ALU.mult)
+        for t in range(1, PACK):
+            gate(t)
+        g_picked = [held([P, PACK, HALF], F32, "g_picked%d" % c, ["d_bytes", "x_picked"][c]) for c in range(2)]
         for c in range(2):
             for t in range(PACK):
                 nc.scalar.activation(
@@ -189,7 +192,7 @@ def tile_picked_hpqkindggtan_none_p_kernel(
 
         steps = [(m, j0, HALF) for m in range(TILES) for j0 in (0, HALF)][:-1]
         steps.extend([(TILES - 1, HALF, QUARTER), (TILES - 1, HALF + QUARTER, QUARTER)])
-        shared = [(0, 1), (1, 1)]
+        shared = [(0, 0), (0, 1)]
 
         def finish(m, j0, width, largest, squashed):
             result = ring.tile([P, width], F32, name="result", tag="result", bufs=3)

@@ -2,7 +2,7 @@ from contextlib import ExitStack
 
 import concourse.mybir as mybir
 
-K, T, S, N, G, H, J = 512, 2048, 512, 512, 2048, 512, 512
+K, T, S, N, H, J = 512, 2048, 512, 512, 512, 512
 FLOPS = 2 * K * H * S + 2 * H * N * S
 
 F32 = mybir.dt.float32
@@ -17,13 +17,15 @@ ACT = mybir.ActivationFunctionType
 
 P = 128
 PACK = 4
-HALF = 256
-QUARTER = 128
+BLOCK_PARTITIONS = 8
+QUADRANT = 32
+HALF = S // 2
+QUARTER = S // 4
 MEMBERS = 4
 PER_COLUMN = 16
-PICK = QUARTER * MEMBERS
-WINDOW = PICK + PER_COLUMN
 TILES = N // P
+WINDOW = HALF * MEMBERS + PER_COLUMN
+LAG = 2
 
 
 def tile_picked_hpqkindggtan_none_p_kernel(
@@ -50,7 +52,7 @@ def tile_picked_hpqkindggtan_none_p_kernel(
         def load_scales(src, name, engine, queue):
             tile = held([P, T], U8, name, name)
             engine.memset(tile[:].bitcast(I32), 0)
-            queue.dma_start(tile[0:P:8, :].bitcast(I32), src[0].bitcast(I32))
+            queue.dma_start(tile[0:P:BLOCK_PARTITIONS, :].bitcast(I32), src[0].bitcast(I32))
             return tile
 
         def load_words(src, name):
@@ -83,7 +85,7 @@ def tile_picked_hpqkindggtan_none_p_kernel(
         nc.gpsimd.tensor_scalar(gain16[:], gain[:], 0.0625, 0.0, ALU.mult, ALU.add)
         h2_rows = [held([P, WINDOW], F32, "h2_rows%d" % m, "h2_rows%d" % m) for m in range(TILES)]
         for m in range(TILES):
-            nc.gpsimd.memset(h2_rows[m][:, S:], 0.0)
+            nc.gpsimd.memset(h2_rows[m][:, 2 * S :], 0.0)
 
         picked_bytes = held([P, H + S], U8, "picked_bytes", "picked_bytes")
         nc.vector.tensor_copy(picked_bytes[:, :H], d_bytes[:].indirect(k1_list[:]))
@@ -94,9 +96,10 @@ def tile_picked_hpqkindggtan_none_p_kernel(
             picked_bytes[:, :H].rearrange("p (c i t) -> p c t i", t=PACK, i=16),
         )
         nc.vector.tensor_copy(dealt_bytes[:, H:].bitcast(I32), picked_bytes[:, H:].bitcast(I32))
-        for q in range(4):
+        for q0 in range(0, P, QUADRANT):
             nc.sync.dma_start(
-                planes[32 * q : 32 * q + 4, :].bitcast(I32), dealt_bytes[32 * q : 32 * q + 32 : 8, :].bitcast(I32)
+                planes[q0 : q0 + QUADRANT // BLOCK_PARTITIONS, :].bitcast(I32),
+                dealt_bytes[q0 : q0 + QUADRANT : BLOCK_PARTITIONS, :].bitcast(I32),
             )
 
         tab_rows.append(load_tab(3, "x_bytes"))
@@ -114,7 +117,9 @@ def tile_picked_hpqkindggtan_none_p_kernel(
             nc.vector.tensor_copy(x_picked[:, j0 : j0 + HALF], x_table[:].indirect(entries(offs_list, j0, HALF)))
 
         h_banks = [psum.tile([P, S], F32, name="bank", tag="bank") for t in range(PACK)]
-        for t, j0 in [(0, 0), (1, 0), (0, HALF), (1, HALF), (2, 0), (2, HALF), (3, 0), (3, HALF)]:
+        passes = [(t, j0) for j0 in (0, HALF) for t in range(2)]
+        passes.extend([(t, j0) for t in range(2, PACK) for j0 in (0, HALF)])
+        for t, j0 in passes:
             cols = slice(t * P, (t + 1) * P)
             nc.tensor.matmul_mx(
                 out=h_banks[t][:, j0 : j0 + HALF], lhsT=d_dealt[:, cols].bitcast(FP8X4), lhsT_scale=planes[:, cols],
@@ -122,7 +127,7 @@ def tile_picked_hpqkindggtan_none_p_kernel(
                 start=True, stop=True,
             )
 
-        tab_picked = [held([P, S], F32, "tab_picked%d" % t, "tab_picked%d" % t) for t in range(PACK)]
+        tab_picked = [h2_rows[t][:, S : 2 * S] for t in range(PACK)]
         for t in range(PACK):
             for j0 in range(0, S, HALF):
                 nc.scalar.activation(
@@ -135,7 +140,7 @@ def tile_picked_hpqkindggtan_none_p_kernel(
 
         def gate(t):
             nc.vector.scalar_tensor_tensor(
-                gated[:, t, :], h_banks[t][:], gain16[:, t : t + 1], tab_picked[t][:], ALU.mult, ALU.mult
+                gated[:, t, :], h_banks[t][:], gain16[:, t : t + 1], tab_picked[t], ALU.mult, ALU.mult
             )
 
         gate(0)
@@ -192,40 +197,39 @@ def tile_picked_hpqkindggtan_none_p_kernel(
 
         steps = [(m, j0, HALF) for m in range(TILES) for j0 in (0, HALF)][:-1]
         steps.extend([(TILES - 1, HALF, QUARTER), (TILES - 1, HALF + QUARTER, QUARTER)])
-        shared = [(0, 0), (0, 1)]
 
         def finish(m, j0, width, largest, squashed):
             result = ring.tile([P, width], F32, name="result", tag="result", bufs=3)
             nc.vector.tensor_tensor(result[:], largest[:], squashed[:], ALU.mult)
             nc.sync.dma_start(out[m * P : (m + 1) * P, j0 : j0 + width], result[:])
 
-        pending = None
+        pending = []
         for m, j0, width in steps:
             if j0 == 0 and m + 1 < TILES:
                 evict(m + 1, 1)
             count = width * MEMBERS
-            first = j0 * MEMBERS
             members = ring.tile([P, count], F32, name="members", tag="members")
-            for at in range(0, count, PICK):
-                picked = h2_rows[m][:].indirect(entries(n3_list, first + at, PICK))
-                if (m, (first + at) // PICK) in shared:
-                    nc.vector.tensor_copy(members[:, at : at + PICK], picked)
-                else:
-                    nc.scalar.activation(members[:, at : at + PICK], picked, ACT.Copy)
+            picked = h2_rows[m][:].indirect(entries(n3_list, j0 * MEMBERS, count))
+            if (m, j0) == (0, 0):
+                nc.vector.tensor_copy(members[:], picked)
+            else:
+                nc.scalar.activation(members[:], picked, ACT.Copy)
             quads = members[:].rearrange("p (j a b) -> p j a b", a=2, b=2)
             high = ring.tile([P, width, 2], F32, name="high", tag="high")
             low = ring.tile([P, width, 2], F32, name="low", tag="low")
             nc.vector.tensor_tensor(high[:], quads[:, :, 0, :], quads[:, :, 1, :], ALU.max)
             nc.vector.tensor_tensor(low[:], quads[:, :, 0, :], quads[:, :, 1, :], ALU.min)
-            largest = ring.tile([P, width], F32, name="largest", tag="largest", bufs=3)
+            largest = ring.tile([P, width], F32, name="largest", tag="largest", bufs=LAG + 2)
             smallest = ring.tile([P, width], F32, name="smallest", tag="smallest")
             nc.vector.tensor_tensor(largest[:], high[:, :, 0], high[:, :, 1], ALU.max)
             nc.vector.tensor_tensor(smallest[:], low[:, :, 0], low[:, :, 1], ALU.min)
-            if pending is not None:
-                finish(*pending)
+            if len(pending) == LAG:
+                finish(*pending[0])
+                pending = pending[1:]
             gap = ring.tile([P, width], F32, name="gap", tag="gap")
             nc.vector.tensor_tensor(gap[:], h2_rows[m][:, j0 : j0 + width], smallest[:], ALU.subtract)
-            squashed = ring.tile([P, width], F32, name="squashed", tag="squashed")
+            squashed = ring.tile([P, width], F32, name="squashed", tag="squashed", bufs=LAG + 1)
             nc.scalar.activation(squashed[:], gap[:], ACT.Tanh)
-            pending = (m, j0, width, largest, squashed)
-        finish(*pending)
+            pending.append((m, j0, width, largest, squashed))
+        for state in pending:
+            finish(*state)

from contextlib import ExitStack

import concourse.mybir as mybir

K, T, S, N, H, J = 512, 2048, 512, 512, 512, 512
FLOPS = 2 * K * H * S + 2 * H * N * S

F32 = mybir.dt.float32
BF16 = mybir.dt.bfloat16
I32 = mybir.dt.int32
U32 = mybir.dt.uint32
U16 = mybir.dt.uint16
U8 = mybir.dt.uint8
FP8X4 = mybir.dt.float8_e4m3fn_x4
ALU = mybir.AluOpType
ACT = mybir.ActivationFunctionType

P = 128
PACK = 4
BLOCK_PARTITIONS = 8
QUADRANT = 32
HALF = S // 2
QUARTER = S // 4
MEMBERS = 4
PER_COLUMN = 16
TILES = N // P
WINDOW = HALF * MEMBERS + PER_COLUMN
LAG = 2


def tile_picked_hpqkindggtan_none_p_kernel(
    tc, x_words, x_scales, d_words, d_scales, tab, gn, w1, offs, k1, n1, n2, n3, out
):
    nc = tc.nc
    with ExitStack() as ctx:
        lists = ctx.enter_context(tc.tile_pool(name="lists", bufs=1))
        keep = ctx.enter_context(tc.tile_pool(name="keep", bufs=1))
        ring = ctx.enter_context(tc.tile_pool(name="ring", bufs=2))
        psum = ctx.enter_context(tc.psum_pool(name="psum", bufs=8))

        def held(shape, dtype, name, tag):
            return keep.tile(shape, dtype, name=name, tag=tag, align_bytes=64)

        def entries(list_tile, first, count):
            return list_tile[:, first // PER_COLUMN : (first + count) // PER_COLUMN]

        def load_list(src, name):
            tile = lists.tile(list(src.shape), U16, name=name)
            nc.sync.dma_start(tile[:], src)
            return tile

        def load_scales(src, name, engine, queue):
            tile = held([P, T], U8, name, name)
            engine.memset(tile[:].bitcast(I32), 0)
            queue.dma_start(tile[0:P:BLOCK_PARTITIONS, :].bitcast(I32), src[0].bitcast(I32))
            return tile

        def load_words(src, name):
            tile = held([P, T], U32, name, name)
            nc.sync.dma_start(tile[:].bitcast(I32), src[0].rearrange("p n r -> p (n r)").bitcast(I32))
            return tile

        def load_tab(t, tag):
            tile = held([P, J], F32, "tab%d" % t, tag)
            nc.sync.dma_start(tile[:], tab.rearrange("(p t) n -> p t n", t=PACK)[:, t, :])
            return tile

        d_bytes = load_scales(d_scales, "d_bytes", nc.vector, nc.sync)
        x_bytes = load_scales(x_scales, "x_bytes", nc.gpsimd, nc.scalar)
        k1_list = load_list(k1, "k1_list")
        offs_list = load_list(offs, "offs_list")
        n1_list = load_list(n1, "n1_list")
        n2_list = load_list(n2, "n2_list")
        n3_list = load_list(n3, "n3_list")
        d_table = load_words(d_words, "d_table")
        tab_rows = [load_tab(0, "tab0"), load_tab(1, "tab1")]
        x_table = load_words(x_words, "x_table")
        tab_rows.append(load_tab(2, "tab2"))

        planes = held([P, H + S], U8, "planes", "planes")
        nc.gpsimd.memset(planes[:].bitcast(I32), 0)
        gain = held([P, PACK], F32, "gain", "gain")
        nc.gpsimd.dma_start(gain[:], gn.rearrange("(p t) o -> p (t o)", t=PACK))
        gain16 = held([P, PACK], F32, "gain16", "gain16")
        nc.gpsimd.tensor_scalar(gain16[:], gain[:], 0.0625, 0.0, ALU.mult, ALU.add)
        h2_rows = [held([P, WINDOW], F32, "h2_rows%d" % m, "h2_rows%d" % m) for m in range(TILES)]
        for m in range(TILES):
            nc.gpsimd.memset(h2_rows[m][:, 2 * S :], 0.0)

        picked_bytes = held([P, H + S], U8, "picked_bytes", "picked_bytes")
        nc.vector.tensor_copy(picked_bytes[:, :H], d_bytes[:].indirect(k1_list[:]))
        nc.vector.tensor_copy(picked_bytes[:, H:], x_bytes[:].indirect(offs_list[:]))
        dealt_bytes = held([P, H + S], U8, "dealt_bytes", "dealt_bytes")
        nc.vector.tensor_copy(
            dealt_bytes[:, :H].rearrange("p (t c i) -> p c t i", t=PACK, i=16),
            picked_bytes[:, :H].rearrange("p (c i t) -> p c t i", t=PACK, i=16),
        )
        nc.vector.tensor_copy(dealt_bytes[:, H:].bitcast(I32), picked_bytes[:, H:].bitcast(I32))
        for q0 in range(0, P, QUADRANT):
            nc.sync.dma_start(
                planes[q0 : q0 + QUADRANT // BLOCK_PARTITIONS, :].bitcast(I32),
                dealt_bytes[q0 : q0 + QUADRANT : BLOCK_PARTITIONS, :].bitcast(I32),
            )

        tab_rows.append(load_tab(3, "x_bytes"))
        d_picked = held([P, H], U32, "d_picked", "picked_bytes")
        nc.vector.tensor_copy(d_picked[:], d_table[:].indirect(k1_list[:]))
        w_raw = held([P, PACK, N], F32, "w_raw", "d_table")
        nc.sync.dma_start(w_raw[:], w1.rearrange("(p t) n -> p t n", t=PACK))
        d_dealt = held([P, H], U32, "d_dealt", "d_dealt")
        nc.vector.tensor_copy(
            d_dealt[:].bitcast(I32).rearrange("p (t c i) -> p c t i", t=PACK, i=4),
            d_picked[:].bitcast(I32).rearrange("p (c i t) -> p c t i", t=PACK, i=4),
        )
        x_picked = held([P, S], U32, "x_picked", "x_picked")
        for j0 in range(0, S, HALF):
            nc.vector.tensor_copy(x_picked[:, j0 : j0 + HALF], x_table[:].indirect(entries(offs_list, j0, HALF)))

        h_banks = [psum.tile([P, S], F32, name="bank", tag="bank") for t in range(PACK)]
        passes = [(t, j0) for j0 in (0, HALF) for t in range(2)]
        passes.extend([(t, j0) for t in range(2, PACK) for j0 in (0, HALF)])
        for t, j0 in passes:
            cols = slice(t * P, (t + 1) * P)
            nc.tensor.matmul_mx(
                out=h_banks[t][:, j0 : j0 + HALF], lhsT=d_dealt[:, cols].bitcast(FP8X4), lhsT_scale=planes[:, cols],
                rhs=x_picked[:, j0 : j0 + HALF].bitcast(FP8X4), rhs_scale=planes[:, H + j0 : H + j0 + HALF],
                start=True, stop=True,
            )

        tab_picked = [h2_rows[t][:, S : 2 * S] for t in range(PACK)]
        for t in range(PACK):
            for j0 in range(0, S, HALF):
                nc.scalar.activation(
                    tab_picked[t][:, j0 : j0 + HALF], tab_rows[t][:].indirect(entries(n1_list, j0, HALF)), ACT.Copy
                )

        g_tags = ["x_bytes", "tab0", "tab1", "tab2"]
        g_rows = [held([P, S], F32, "g_rows%d" % t, g_tags[t]) for t in range(PACK)]
        gated = held([P, PACK, S], F32, "gated", "gated")

        def gate(t):
            nc.vector.scalar_tensor_tensor(
                gated[:, t, :], h_banks[t][:], gain16[:, t : t + 1], tab_picked[t], ALU.mult, ALU.mult
            )

        gate(0)
        nc.scalar.activation(g_rows[0][:], h_banks[0][:], ACT.Copy, scale=gain16[:, 0:1])
        for t in range(1, PACK):
            nc.vector.tensor_scalar(g_rows[t][:], h_banks[t][:], gain16[:, t : t + 1], None, ALU.mult)
        for t in range(1, PACK):
            gate(t)
        g_picked = [held([P, PACK, HALF], F32, "g_picked%d" % c, ["d_bytes", "x_picked"][c]) for c in range(2)]
        for c in range(2):
            for t in range(PACK):
                nc.scalar.activation(
                    g_picked[c][:, t, :], g_rows[t][:].indirect(entries(n2_list, c * HALF, HALF)),
                    ACT.Copy, scale=-0.5,
                )

        w_grouped = held([P, N * PACK], BF16, "w_grouped", "grouped")
        nc.gpsimd.tensor_scalar(
            w_grouped[:].rearrange("p (n t) -> p n t", t=PACK), w_raw[:].rearrange("p t n -> p n t"),
            1.0, 0.0, ALU.mult, ALU.add,
        )
        w_codes = held([P, N], U32, "w_codes", "w_codes")
        w_plane = held([P, N], U8, "w_plane", "w_plane")
        nc.vector.quantize_mx(out=w_codes[:].bitcast(FP8X4), scales=w_plane[:], in_=w_grouped[:])

        h2_banks = {}
        for c in range(2):
            cols = slice(c * HALF, (c + 1) * HALF)
            z_grouped = held([P, HALF * PACK], BF16, "z_grouped", "grouped")
            nc.vector.tensor_tensor(
                z_grouped[:].rearrange("p (c i t) -> p c t i", t=PACK, i=2),
                g_picked[c][:].rearrange("p t (c i) -> p c t i", i=2),
                gated[:, :, cols].rearrange("p t (c i) -> p c t i", i=2),
                ALU.add,
            )
            z_codes = ring.tile([P, HALF], U32, name="z_codes", align_bytes=64)
            z_plane = ring.tile([P, HALF], U8, name="z_plane", align_bytes=64)
            nc.vector.quantize_mx(out=z_codes[:].bitcast(FP8X4), scales=z_plane[:], in_=z_grouped[:])
            for m in range(TILES):
                bank = psum.tile([P, HALF], F32, name="bank", tag="bank")
                rows = slice(m * P, (m + 1) * P)
                nc.tensor.matmul_mx(
                    out=bank[:], lhsT=w_codes[:, rows].bitcast(FP8X4), lhsT_scale=w_plane[:, rows],
                    rhs=z_codes[:].bitcast(FP8X4), rhs_scale=z_plane[:], start=True, stop=True,
                )
                h2_banks[(m, c)] = bank

        def evict(m, c):
            nc.scalar.activation(h2_rows[m][:, c * HALF : (c + 1) * HALF], h2_banks[(m, c)][:], ACT.Copy)

        for m in range(TILES):
            evict(m, 0)
        evict(0, 1)

        steps = [(m, j0, HALF) for m in range(TILES) for j0 in (0, HALF)][:-1]
        steps.extend([(TILES - 1, HALF, QUARTER), (TILES - 1, HALF + QUARTER, QUARTER)])

        def finish(m, j0, width, largest, squashed):
            result = ring.tile([P, width], F32, name="result", tag="result", bufs=3)
            nc.vector.tensor_tensor(result[:], largest[:], squashed[:], ALU.mult)
            nc.sync.dma_start(out[m * P : (m + 1) * P, j0 : j0 + width], result[:])

        pending = []
        for m, j0, width in steps:
            if j0 == 0 and m + 1 < TILES:
                evict(m + 1, 1)
            count = width * MEMBERS
            members = ring.tile([P, count], F32, name="members", tag="members")
            picked = h2_rows[m][:].indirect(entries(n3_list, j0 * MEMBERS, count))
            if (m, j0) == (0, 0):
                nc.vector.tensor_copy(members[:], picked)
            else:
                nc.scalar.activation(members[:], picked, ACT.Copy)
            quads = members[:].rearrange("p (j a b) -> p j a b", a=2, b=2)
            high = ring.tile([P, width, 2], F32, name="high", tag="high")
            low = ring.tile([P, width, 2], F32, name="low", tag="low")
            nc.vector.tensor_tensor(high[:], quads[:, :, 0, :], quads[:, :, 1, :], ALU.max)
            nc.vector.tensor_tensor(low[:], quads[:, :, 0, :], quads[:, :, 1, :], ALU.min)
            largest = ring.tile([P, width], F32, name="largest", tag="largest", bufs=LAG + 2)
            smallest = ring.tile([P, width], F32, name="smallest", tag="smallest")
            nc.vector.tensor_tensor(largest[:], high[:, :, 0], high[:, :, 1], ALU.max)
            nc.vector.tensor_tensor(smallest[:], low[:, :, 0], low[:, :, 1], ALU.min)
            if len(pending) == LAG:
                finish(*pending[0])
                pending = pending[1:]
            gap = ring.tile([P, width], F32, name="gap", tag="gap")
            nc.vector.tensor_tensor(gap[:], h2_rows[m][:, j0 : j0 + width], smallest[:], ALU.subtract)
            squashed = ring.tile([P, width], F32, name="squashed", tag="squashed", bufs=LAG + 1)
            nc.scalar.activation(squashed[:], gap[:], ACT.Tanh)
            pending.append((m, j0, width, largest, squashed))
        for state in pending:
            finish(*state)
